import numpy as np
import ml_dtypes


def mxq(x, axis, fmt="e4m3"):
    dtype, down = {"e4m3": (ml_dtypes.float8_e4m3fn, 7), "e5m2": (ml_dtypes.float8_e5m2, 14)}[fmt]
    v = np.moveaxis(np.asarray(x, np.float32).astype(ml_dtypes.bfloat16).astype(np.float64), axis, -1)
    blocks = v.reshape(v.shape[:-1] + (-1, 32))
    amax = np.abs(blocks).max(-1, keepdims=True)
    byte = np.maximum(np.where(amax > 0, np.frexp(amax)[1] - 1 + 127, 0) - down, 1)
    scale = np.exp2(byte - 127.0)
    codes = (blocks / scale).astype(np.float32).astype(dtype).astype(np.float64)
    return np.moveaxis((codes * scale).reshape(v.shape), -1, axis)


WIDE = False


def mx_kscale(k):
    if not WIDE:
        return np.ones(k)
    levels = np.array([10, -10, 5, -5, 0])
    if k % 512:
        return np.exp2(np.random.permutation(np.resize(levels, k // 32))).repeat(32)
    a = np.empty((k // 512, 16))
    for p in range(k // 512):
        a[p, :8] = np.random.permutation(np.resize(levels, 8))
        for g in range(8):
            far = levels[np.abs(levels - a[p, g]) >= 10]
            a[p, g + 8] = far[np.random.randint(len(far))]
    return np.exp2(a.ravel()).repeat(32)


def f64(x):
    return np.asarray(x).astype(np.float64)


def striped(idx):
    return np.tile(idx.reshape(-1, 16).T, (8, 1)).astype(np.uint16)


def unstriped(offs):
    return offs[:16].T.reshape(-1).astype(np.int64)


E2M1 = np.array([0.0, 0.5, 1.0, 1.5, 2.0, 3.0, 4.0, 6.0, -0.0, -0.5, -1.0, -1.5, -2.0, -3.0, -4.0, -6.0])


def pack_weight(w, fmt):
    k, n = w.shape
    w = f64(np.asarray(w, np.float32).astype(ml_dtypes.bfloat16)).reshape(k // 32, 32, n)
    amax = np.abs(w).max(1)
    if fmt == "e4m3":
        byte = np.frexp(amax)[1] - 1 + 127 - 7
    else:
        mant, ex = np.frexp(amax / 6.0)
        byte = np.where(mant > 0.5, ex, ex - 1) + 127
    byte = np.clip(np.where(amax > 0, byte, 1), 1, 254)
    scaled = (w * np.exp2(127.0 - byte)[:, None, :]).reshape(k, n).astype(np.float32)
    by_word = np.ascontiguousarray(scaled.reshape(k // 512, 128, 4, n).transpose(0, 1, 3, 2))
    if fmt == "e4m3":
        words = by_word.astype(ml_dtypes.float8_e4m3fn).view(np.uint8)
    else:
        c = by_word.astype(ml_dtypes.float4_e2m1fn).view(np.uint8) & 0xF
        words = (c[..., 0::2] | (c[..., 1::2] << 4)).reshape(k // 512, 128, 2 * n)
    return np.ascontiguousarray(words), np.ascontiguousarray(byte.astype(np.uint8).reshape(k // 512, 16, n))


def unpack_weight(words, scales, fmt):
    g, _, n = scales.shape
    words = np.ascontiguousarray(words).reshape(g, 128, n, -1)
    if fmt == "e4m3":
        vals = words.view(ml_dtypes.float8_e4m3fn).astype(np.float64)
    else:
        nib = np.empty((g, 128, n, 4), np.uint8)
        nib[..., 0::2] = words & 0xF
        nib[..., 1::2] = words >> 4
        vals = E2M1[nib]
    vals = vals * np.repeat(np.exp2(scales.astype(np.float64) - 127.0), 8, axis=1)[..., None]
    return vals.transpose(0, 1, 3, 2).reshape(g * 512, n)


def gelu(v):
    return 0.5 * v * (1.0 + np.tanh(np.sqrt(2.0 / np.pi) * (v + 0.044715 * v**3)))


def bf(x):
    return np.asarray(x, np.float32).astype(ml_dtypes.bfloat16)


def planes(Y):
    n, m = Y.shape
    b = f64(bf(Y)).reshape(n // 32, 32, m)
    amax = np.abs(b).max(1)
    byte = np.clip(np.where(amax > 0, np.frexp(amax)[1] - 1 + 127 - 7, 1), 1, 254)
    codes = (b * np.exp2(127.0 - byte)[:, None, :]).reshape(n, m).astype(np.float32).astype(ml_dtypes.float8_e4m3fn).view(np.uint8)
    words = codes.reshape(n // 512, 128, 4, m).transpose(0, 1, 3, 2)
    return np.ascontiguousarray(words), np.ascontiguousarray(byte.astype(np.uint8).reshape(n // 512, 16, m))


K, T, S, H, T2, P, N = 1024, 4096, 1024, 512, 2048, 1024, 384

def setup_inputs():
    n = np.random.standard_normal
    s = mx_kscale(K)[:, None]
    u = mx_kscale(H)[:, None]
    d = {}
    d["tab_words"], d["tab_scales"] = pack_weight(n((K, T)) * s, "e4m3")
    d["offs"] = striped(np.random.permutation(T)[:S])
    d["offs2"] = striped(np.random.permutation(T2)[:S])
    d["offs3"] = striped(np.random.permutation(T2)[:P])
    d["w1"] = (1.5 * n((K, H)) / s / K**0.5).astype(np.float32)
    d["gain"] = (np.exp(0.3 * n(H)) * u[:, 0]).astype(np.float32)
    d["w2_words"], d["w2_scales"] = pack_weight(1.4 * n((H, H)) / u * u.T / H**0.5, "e2m1")
    d["wgs"] = np.exp(0.3 * n((128, S))).astype(np.float32)
    d["page0"] = (1.2 * n((H, T2)) * u).astype(np.float32)
    d["b3"] = (0.8 * n(H) * u[:, 0]).astype(np.float32)
    d["w3"] = (n((H, N)) / u / H**0.5).astype(np.float32)
    d["low"] = (0.7 * n(N)).astype(np.float32)
    return d

def reference(tab_words, tab_scales, offs, offs2, offs3, w1, gain, w2_words, w2_scales, wgs, page0, b3, w3, low):
    v = unpack_weight(tab_words, tab_scales, "e4m3")[:, unstriped(offs)]
    base = mxq(f64(w1), 0, "e4m3").T @ v
    bent = np.tanh(base) * f64(gain)[:, None]
    w2 = unpack_weight(w2_words, w2_scales, "e2m1")
    resp = w2.T @ mxq(bent, 0, "e4m3")
    h = base * resp
    page = f64(page0).copy()
    page[:, unstriped(offs2)] = np.tile(f64(wgs), (H // 128, 1)) * h
    x = page[:, unstriped(offs3)] + f64(b3)[:, None]
    y = mxq(f64(w3), 0, "e4m3").T @ mxq(x, 0, "e4m3")
    y = np.maximum(y, f64(low)[:, None])
    words, scales = planes(page)
    return y, page, words, scales

@@ -1,0 +1,299 @@
+from contextlib import ExitStack
+
+import concourse.mybir as mybir
+
+K, T, S, H, T2, NREAD, N = 1024, 4096, 1024, 512, 2048, 1024, 384
+FLOPS = 2 * K * H * S + 2 * H * H * S + 2 * H * N * NREAD
+
+F32 = mybir.dt.float32
+BF16 = mybir.dt.bfloat16
+I32 = mybir.dt.int32
+U32 = mybir.dt.uint32
+U16 = mybir.dt.uint16
+U8 = mybir.dt.uint8
+FP8X4 = mybir.dt.float8_e4m3fn_x4
+FP4X4 = mybir.dt.float4_e2m1fn_x4
+MULT = mybir.AluOpType.mult
+ACT = mybir.ActivationFunctionType
+
+P = 128
+PACK = 4
+HALF = 512
+CHUNK = 256
+BLOCK = 128
+
+
+def tile_list_polar_cell_tuning_kernel(
+    tc, tab_words, tab_scales, offs, offs2, offs3, w1, gain, w2_words, w2_scales, wgs, page0, b3, w3, low,
+    out_0, out_1, out_2, out_3,
+):
+    nc = tc.nc
+    passes = K // (P * PACK)
+    with ExitStack() as ctx:
+        sb = ctx.enter_context(tc.tile_pool(name="sb", bufs=1))
+        ps = ctx.enter_context(tc.psum_pool(name="ps", bufs=1))
+
+        def tile(name, shape, dtype, tag="", bufs=1):
+            return sb.tile(shape, dtype, name=name, tag=tag or name, bufs=bufs, align_bytes=64)
+
+        def bank(b, name, shape):
+            return ps.tile(shape, F32, name=name, tag="bank%d" % b)
+
+        def entries(lst, j0, count):
+            return lst[:, j0 // 16 : (j0 + count) // 16]
+
+        idx1 = sb.tile([P, S // 16], U16, name="idx1")
+        idx2 = sb.tile([P, S // 16], U16, name="idx2")
+        idx3 = sb.tile([P, NREAD // 16], U16, name="idx3")
+        nc.sync.dma_start(idx1[:], offs)
+
+        tab_sc = tile("tab_sc", [P, T], U8)
+        w2_sc_raw = tile("w2_sc_raw", [P, H], U8)
+        nc.vector.memset(tab_sc[:].bitcast(I32), 0)
+        nc.vector.memset(w2_sc_raw[:].bitcast(I32), 0)
+
+        w2_raw = tile("w2_raw", [P, 2 * H], U8)
+        nc.sync.dma_start(w2_raw[:].bitcast(I32), w2_words[0].bitcast(I32))
+        gain_sb = tile("gain_sb", [P, PACK], F32)
+        nc.sync.dma_start(gain_sb[:], gain.rearrange("(p t) -> p t", t=PACK))
+        nc.sync.dma_start(idx2[:], offs2)
+        nc.sync.dma_start(idx3[:], offs3)
+        w1_raw = []
+        for a in range(passes):
+            raw = tile("w1_raw%d" % a, [P, PACK, H], F32, tag="big8", bufs=2)
+            nc.sync.dma_start(raw[:], w1[512 * a : 512 * (a + 1), :].rearrange("(p j) c -> p j c", j=PACK))
+            w1_raw.append(raw)
+            if a == 0:
+                for q in range(4):
+                    nc.sync.dma_start(
+                        tab_sc[32 * q : 32 * q + 4 * passes, :].bitcast(I32),
+                        tab_scales[:, 4 * q : 4 * q + 4, :].bitcast(I32),
+                    )
+        b3_sb = tile("b3_sb", [P, PACK], F32)
+        tab = []
+        for a in range(passes):
+            words = tile("tab%d" % a, [P, T], U32)
+            nc.sync.dma_start(words[:].bitcast(I32), tab_words[a].rearrange("p c i -> p (c i)").bitcast(I32))
+            tab.append(words)
+            if a == 0:
+                nc.sync.dma_start(b3_sb[:], b3.rearrange("(p t) -> p t", t=PACK))
+        for q in range(4):
+            nc.sync.dma_start(
+                w2_sc_raw[32 * q : 32 * q + 4, :].bitcast(I32), w2_scales[0, 4 * q : 4 * q + 4, :].bitcast(I32)
+            )
+
+        wgs_rows = wgs.rearrange("(p t) j -> p t j", t=PACK)
+        page_rows = page0.rearrange("(p t) c -> p t c", t=PACK)
+        out1_rows = out_1.rearrange("(p t) c -> p t c", t=PACK)
+        wgs_sb, page = [], []
+        low_sb = tile("low_sb", [P, N // P], F32)
+        w3_raw = tile("w3_raw", [P, PACK, N], F32)
+        for t in range(PACK):
+            factors = tile("wgs%d" % t, [P, S], F32)
+            for q in (0, 2, 1, 3):
+                nc.sync.dma_start(factors[32 * q : 32 * (q + 1), :], wgs_rows[:, t, :])
+            wgs_sb.append(factors)
+            cells = tile("page%d" % t, [P, T2], F32)
+            nc.sync.dma_start(cells[:], page_rows[:, t, :])
+            page.append(cells)
+            if t == 1:
+                with nc.allow_non_contiguous_dma(reason="one floor value a partition"):
+                    nc.sync.dma_start(low_sb[:], low.rearrange("(u p) -> p u", p=P))
+                nc.sync.dma_start(w3_raw[:], w3.rearrange("(p j) c -> p j c", j=PACK))
+
+        warm = tile("warm", [P, 1], F32)
+        nc.vector.memset(warm[:], 0.0)
+        warm_out = tile("warm_out", [P, 1], F32)
+        nc.scalar.activation(warm_out[:], warm[:], ACT.Tanh)
+
+        w2_codes = tile("w2_codes", [P, PACK, P, 2], U8)
+        w2_sc = tile("w2_sc", [P, PACK, P], U8)
+        nc.vector.tensor_copy(
+            w2_codes[:].rearrange("p t m b -> p m t b"), w2_raw[:].rearrange("p (m t b) -> p m t b", t=PACK, b=2)
+        )
+        w1_codes, w1_sc = [], []
+        for a in range(passes):
+            grouped = tile("w1_bf%d" % a, [P, PACK, P, PACK], BF16, tag="mid4", bufs=2)
+            nc.scalar.copy(
+                grouped[:].rearrange("p t m j -> p m j t"), w1_raw[a][:].rearrange("p j (m t) -> p m j t", t=PACK)
+            )
+            codes = tile("w1_codes%d" % a, [P, H], U32)
+            scales = tile("w1_sc%d" % a, [P, H], U8)
+            nc.vector.quantize_mx(codes[:].bitcast(FP8X4), scales[:], grouped[:].rearrange("p t m j -> p (t m j)"))
+            w1_codes.append(codes)
+            w1_sc.append(scales)
+
+        v_sc = tile("v_sc", [P, S], U8)
+        nc.vector.tensor_copy(v_sc[:], tab_sc[:].indirect(idx1[:]))
+        v = [[None, None] for a in range(passes)]
+        for a in range(passes):
+            for h in range(2):
+                v[a][h] = tile("v%d_%d" % (a, h), [P, HALF], U32)
+                nc.vector.tensor_copy(v[a][h][:], tab[a][:].indirect(entries(idx1, HALF * h, HALF)))
+        nc.vector.tensor_copy(
+            w2_sc[:].rearrange("p t m -> p m t"), w2_sc_raw[:].rearrange("p (m t) -> p m t", t=PACK)
+        )
+
+        def first_product(out, a, t, h, j0, count, start, stop):
+            nc.tensor.matmul_mx(
+                out,
+                lhsT=w1_codes[a][:, P * t : P * (t + 1)].bitcast(FP8X4),
+                lhsT_scale=w1_sc[a][:, P * t : P * (t + 1)],
+                rhs=v[a][h][:, j0 : j0 + count].bitcast(FP8X4),
+                rhs_scale=v_sc[4 * a : P, HALF * h + j0 : HALF * h + j0 + count],
+                start=start,
+                stop=stop,
+            )
+
+        def second_product(out, t, codes, scales):
+            nc.tensor.matmul_mx(
+                out,
+                lhsT=w2_codes[:, t, :, :].rearrange("p m b -> p (m b)").bitcast(FP4X4),
+                lhsT_scale=w2_sc[:, t, :],
+                rhs=codes[:].bitcast(FP8X4),
+                rhs_scale=scales[:],
+                start=True,
+                stop=True,
+            )
+
+        def quantise(name, grouped, width):
+            codes = tile(name + "_codes", [P, width], U32)
+            scales = tile(name + "_sc", [P, width], U8)
+            nc.vector.quantize_mx(codes[:].bitcast(FP8X4), scales[:], grouped[:].rearrange("p n t -> p (n t)"))
+            return codes, scales
+
+        def weave(engine_copy, grouped, pairs):
+            engine_copy(
+                grouped[:].rearrange("p n t -> p (n t)").bitcast(F32).rearrange("p (n u) -> p n u", u=2),
+                pairs[:].rearrange("p u n e -> p u (n e)").bitcast(F32).rearrange("p u n -> p n u"),
+            )
+
+        hval = [tile("hval%d" % h, [P, PACK, HALF], F32) for h in range(2)]
+
+        def put(t, h, j0, count):
+            nc.vector.tensor_tensor(
+                page[t][:].indirect(entries(idx2, HALF * h + j0, count)),
+                hval[h][:, t, j0 : j0 + count],
+                wgs_sb[t][:, HALF * h + j0 : HALF * h + j0 + count],
+                MULT,
+            )
+
+        blocks = HALF // BLOCK
+        base0 = [bank(b, "base0_%d" % b, [P, PACK, BLOCK]) for b in range(blocks)]
+        for a in range(passes):
+            for b in range(blocks):
+                for t in range(PACK):
+                    first_product(
+                        base0[b][:, t, :], a, t, 0, BLOCK * b, BLOCK,
+                        a == 0 and t == 0, a == passes - 1 and t == PACK - 1,
+                    )
+        gain_cols = gain_sb[:].unsqueeze(1).to_broadcast([P, BLOCK, PACK])
+        bent0, resp0 = [], []
+        for c in range(HALF // CHUNK):
+            grouped = tile("bent_bf0_%d" % c, [P, CHUNK, PACK], BF16)
+            for i in range(CHUNK // BLOCK):
+                b = c * (CHUNK // BLOCK) + i
+                bentf = tile("tanh0_%d" % b, [P, BLOCK, PACK], F32, tag="f2k", bufs=4)
+                nc.scalar.activation(bentf[:], base0[b][:].rearrange("p t n -> p n t"), ACT.Tanh)
+                nc.vector.tensor_tensor(grouped[:, BLOCK * i : BLOCK * (i + 1), :], bentf[:], gain_cols, MULT)
+            codes, scales = quantise("bent0_%d" % c, grouped, CHUNK)
+            for u in range(2):
+                acc = bank(blocks + 2 * c + u, "resp0_%d_%d" % (c, u), [P, 2, CHUNK])
+                for e in range(2):
+                    second_product(acc[:, e, :], 2 * u + e, codes, scales)
+                resp0.append(acc)
+        for b in range(blocks):
+            nc.scalar.copy(hval[0][:, :, BLOCK * b : BLOCK * (b + 1)], base0[b][:])
+
+        def respond0(c, u):
+            part = hval[0][:, 2 * u : 2 * u + 2, CHUNK * c : CHUNK * (c + 1)]
+            nc.vector.tensor_tensor(part, resp0[2 * c + u][:], part, MULT)
+
+        respond0(0, 0)
+        respond0(0, 1)
+        put(0, 0, 0, CHUNK)
+        respond0(1, 0)
+        respond0(1, 1)
+        put(0, 0, CHUNK, CHUNK)
+
+        pairs = tile("bent_pairs", [P, 2, HALF, 2], BF16)
+        base1 = []
+        for t in range(PACK):
+            acc = bank(t, "base1_%d" % t, [P, HALF])
+            for a in range(passes):
+                first_product(acc[:], a, t, 1, 0, HALF, a == 0, a == passes - 1)
+            bentf = tile("tanh1_%d" % t, [P, HALF], F32, tag="f2k", bufs=4)
+            nc.scalar.activation(bentf[:], acc[:], ACT.Tanh)
+            nc.scalar.activation(pairs[:, t // 2, :, t % 2], bentf[:], ACT.Copy, scale=gain_sb[:, t : t + 1])
+            base1.append(acc)
+        grouped = tile("bent_bf1", [P, HALF, PACK], BF16)
+        weave(nc.scalar.copy, grouped, pairs)
+        for t in range(PACK):
+            nc.scalar.copy(hval[1][:, t, :], base1[t][:])
+        codes, scales = quantise("bent1", grouped, HALF)
+        resp1 = []
+        for t in range(PACK):
+            acc = bank(PACK + t, "resp1_%d" % t, [P, HALF])
+            second_product(acc[:], t, codes, scales)
+            resp1.append(acc)
+        put(1, 0, 0, HALF)
+
+        w3_bf = tile("w3_bf", [P, N, PACK], BF16)
+        nc.scalar.copy(w3_bf[:], w3_raw[:].rearrange("p j c -> p c j"))
+        w3_codes = tile("w3_codes", [P, N], U32)
+        w3_sc = tile("w3_sc", [P, N], U8)
+        for c0, c1 in ((0, 256), (256, N)):
+            nc.vector.quantize_mx(
+                w3_codes[:, c0:c1].bitcast(FP8X4), w3_sc[:, c0:c1], w3_bf[:, c0:c1, :].rearrange("p c j -> p (c j)")
+            )
+
+        cols = T2 // 2
+        page_pairs = [tile("page_pairs%d" % h, [P, 2, cols, 2], BF16) for h in range(2)]
+        x_pairs = [tile("x_pairs%d" % h, [P, 2, HALF, 2], BF16) for h in range(2)]
+        for t in range(PACK):
+            nc.vector.tensor_tensor(hval[1][:, t, :], resp1[t][:], hval[1][:, t, :], MULT)
+            if t >= 2:
+                put(t, 0, 0, HALF)
+            put(t, 1, 0, HALF)
+            nc.sync.dma_start(out1_rows[:, t, :], page[t][:])
+            for h in range(2):
+                picked = tile("picked%d_%d" % (t, h), [P, HALF], F32, tag="picked", bufs=4)
+                nc.vector.tensor_copy(picked[:], page[t][:].indirect(entries(idx3, HALF * h, HALF)))
+                nc.scalar.copy(page_pairs[h][:, t // 2, :, t % 2], page[t][:, cols * h : cols * (h + 1)])
+                nc.scalar.activation(
+                    x_pairs[h][:, t // 2, :, t % 2], picked[:], ACT.Identity, bias=b3_sb[:, t : t + 1]
+                )
+
+        plane_sc = tile("plane_sc", [P, T2], U8)
+        out2_words = out_2[0].rearrange("p c i -> p (c i)").bitcast(I32)
+        for h in range(2):
+            engine_copy = nc.vector.tensor_copy if h == 0 else nc.scalar.copy
+            x_bf = tile("x_bf%d" % h, [P, HALF, PACK], BF16, tag="mid4", bufs=2)
+            page_bf = tile("page_bf%d" % h, [P, cols, PACK], BF16, tag="big8", bufs=2)
+            weave(engine_copy, x_bf, x_pairs[h])
+            weave(engine_copy, page_bf, page_pairs[h])
+            codes, scales = quantise("x%d" % h, x_bf, HALF)
+            plane = tile("plane%d" % h, [P, cols], U32)
+            nc.vector.quantize_mx(
+                plane[:].bitcast(FP8X4), plane_sc[:, cols * h : cols * (h + 1)],
+                page_bf[:].rearrange("p n t -> p (n t)"),
+            )
+            nc.sync.dma_start(out2_words[:, cols * h : cols * (h + 1)], plane[:].bitcast(I32))
+            for u in range(N // P):
+                acc = bank((3 * h + u), "y%d_%d" % (h, u), [P, HALF])
+                nc.tensor.matmul_mx(
+                    acc[:],
+                    lhsT=w3_codes[:, P * u : P * (u + 1)].bitcast(FP8X4),
+                    lhsT_scale=w3_sc[:, P * u : P * (u + 1)],
+                    rhs=codes[:].bitcast(FP8X4),
+                    rhs_scale=scales[:],
+                    start=True,
+                    stop=True,
+                )
+                y = tile("y_sb%d_%d" % (h, u), [P, HALF], F32, tag="f2k", bufs=4)
+                nc.vector.tensor_scalar_max(y[:], acc[:], low_sb[:, u : u + 1])
+                nc.sync.dma_start(out_0[P * u : P * (u + 1), HALF * h : HALF * (h + 1)], y[:])
+        for q in range(4):
+            nc.scalar.dma_start(
+                out_3[0, 4 * q : 4 * q + 4, :].bitcast(I32), plane_sc[32 * q : 32 * q + 4, :].bitcast(I32)
+            )

@@ -51,41 +51,38 @@ def tile_list_polar_cell_tuning_kernel(
         w2_sc_raw = tile("w2_sc_raw", [P, H], U8)
         nc.vector.memset(tab_sc[:].bitcast(I32), 0)
         nc.vector.memset(w2_sc_raw[:].bitcast(I32), 0)
+        for q in range(4):
+            nc.gpsimd.dma_start(
+                tab_sc[32 * q : 32 * q + 4 * passes, :].bitcast(I32),
+                tab_scales[:, 4 * q : 4 * q + 4, :].bitcast(I32),
+            )
+        for q in range(4):
+            nc.gpsimd.dma_start(
+                w2_sc_raw[32 * q : 32 * q + 4, :].bitcast(I32), w2_scales[0, 4 * q : 4 * q + 4, :].bitcast(I32)
+            )
 
-        w2_raw = tile("w2_raw", [P, 2 * H], U8)
-        nc.sync.dma_start(w2_raw[:].bitcast(I32), w2_words[0].bitcast(I32))
         gain_sb = tile("gain_sb", [P, PACK], F32)
         nc.sync.dma_start(gain_sb[:], gain.rearrange("(p t) -> p t", t=PACK))
-        nc.sync.dma_start(idx2[:], offs2)
-        nc.sync.dma_start(idx3[:], offs3)
-        w1_raw = []
-        for a in range(passes):
-            raw = tile("w1_raw%d" % a, [P, PACK, H], F32, tag="big8", bufs=2)
-            nc.sync.dma_start(raw[:], w1[512 * a : 512 * (a + 1), :].rearrange("(p j) c -> p j c", j=PACK))
-            w1_raw.append(raw)
-            if a == 0:
-                for q in range(4):
-                    nc.sync.dma_start(
-                        tab_sc[32 * q : 32 * q + 4 * passes, :].bitcast(I32),
-                        tab_scales[:, 4 * q : 4 * q + 4, :].bitcast(I32),
-                    )
-        b3_sb = tile("b3_sb", [P, PACK], F32)
+        w2_raw = tile("w2_raw", [P, 2 * H], U8)
+        nc.sync.dma_start(w2_raw[:].bitcast(I32), w2_words[0].bitcast(I32))
+        w1_rows = w1.rearrange("(a p j) c -> a p j c", p=P, j=PACK)
+        w1_first = tile("w1_first", [P, PACK, H], F32, tag="big8", bufs=2)
+        nc.sync.dma_start(w1_first[:], w1_rows[0])
         tab = []
         for a in range(passes):
             words = tile("tab%d" % a, [P, T], U32)
             nc.sync.dma_start(words[:].bitcast(I32), tab_words[a].rearrange("p c i -> p (c i)").bitcast(I32))
             tab.append(words)
-            if a == 0:
-                nc.sync.dma_start(b3_sb[:], b3.rearrange("(p t) -> p t", t=PACK))
-        for q in range(4):
-            nc.sync.dma_start(
-                w2_sc_raw[32 * q : 32 * q + 4, :].bitcast(I32), w2_scales[0, 4 * q : 4 * q + 4, :].bitcast(I32)
-            )
+        w1_last = tile("w1_last", [P, 2, PACK, H // 2], F32, tag="big8", bufs=2)
+        for s in range(2):
+            nc.sync.dma_start(w1_last[:, s, :, :], w1_rows[1][:, :, H // 2 * s : H // 2 * (s + 1)])
+        nc.sync.dma_start(idx2[:], offs2)
 
         wgs_rows = wgs.rearrange("(p t) j -> p t j", t=PACK)
         page_rows = page0.rearrange("(p t) c -> p t c", t=PACK)
         out1_rows = out_1.rearrange("(p t) c -> p t c", t=PACK)
         wgs_sb, page = [], []
+        b3_sb = tile("b3_sb", [P, PACK], F32)
         low_sb = tile("low_sb", [P, N // P], F32)
         w3_raw = tile("w3_raw", [P, PACK, N], F32)
         for t in range(PACK):
@@ -96,7 +93,9 @@ def tile_list_polar_cell_tuning_kernel(
             cells = tile("page%d" % t, [P, T2], F32)
             nc.sync.dma_start(cells[:], page_rows[:, t, :])
             page.append(cells)
-            if t == 1:
+            if t == 2:
+                nc.sync.dma_start(idx3[:], offs3)
+                nc.sync.dma_start(b3_sb[:], b3.rearrange("(p t) -> p t", t=PACK))
                 with nc.allow_non_contiguous_dma(reason="one floor value a partition"):
                     nc.sync.dma_start(low_sb[:], low.rearrange("(u p) -> p u", p=P))
                 nc.sync.dma_start(w3_raw[:], w3.rearrange("(p j) c -> p j c", j=PACK))
@@ -108,31 +107,35 @@ def tile_list_polar_cell_tuning_kernel(
 
         w2_codes = tile("w2_codes", [P, PACK, P, 2], U8)
         w2_sc = tile("w2_sc", [P, PACK, P], U8)
-        nc.vector.tensor_copy(
-            w2_codes[:].rearrange("p t m b -> p m t b"), w2_raw[:].rearrange("p (m t b) -> p m t b", t=PACK, b=2)
-        )
-        w1_codes, w1_sc = [], []
-        for a in range(passes):
-            grouped = tile("w1_bf%d" % a, [P, PACK, P, PACK], BF16, tag="mid4", bufs=2)
-            nc.scalar.copy(
-                grouped[:].rearrange("p t m j -> p m j t"), w1_raw[a][:].rearrange("p j (m t) -> p m j t", t=PACK)
-            )
-            codes = tile("w1_codes%d" % a, [P, H], U32)
-            scales = tile("w1_sc%d" % a, [P, H], U8)
-            nc.vector.quantize_mx(codes[:].bitcast(FP8X4), scales[:], grouped[:].rearrange("p t m j -> p (t m j)"))
-            w1_codes.append(codes)
-            w1_sc.append(scales)
+        nc.vector.tensor_copy(w2_codes[:], w2_raw[:].rearrange("p (m t b) -> p t m b", t=PACK, b=2))
+        w1_bf = [tile("w1_bf%d" % a, [P, PACK, P, PACK], BF16, tag="mid4", bufs=2) for a in range(passes)]
+        w1_codes = [tile("w1_codes%d" % a, [P, H], U32) for a in range(passes)]
+        w1_sc = [tile("w1_sc%d" % a, [P, H], U8) for a in range(passes)]
 
+        def deal_w1(engine_copy, a, m0, m1, raw):
+            engine_copy(
+                w1_bf[a][:, :, m0:m1, :].rearrange("p t m j -> p m t j"),
+                raw.rearrange("p j (m t) -> p m t j", t=PACK),
+            )
+
+        def quantise_w1(a):
+            nc.vector.quantize_mx(
+                w1_codes[a][:].bitcast(FP8X4), w1_sc[a][:], w1_bf[a][:].rearrange("p t m j -> p (t m j)")
+            )
+
+        deal_w1(nc.scalar.copy, 0, 0, P, w1_first[:])
+        quantise_w1(0)
         v_sc = tile("v_sc", [P, S], U8)
         nc.vector.tensor_copy(v_sc[:], tab_sc[:].indirect(idx1[:]))
+        nc.vector.tensor_copy(w2_sc[:], w2_sc_raw[:].rearrange("p (m t) -> p t m", t=PACK))
         v = [[None, None] for a in range(passes)]
         for a in range(passes):
             for h in range(2):
                 v[a][h] = tile("v%d_%d" % (a, h), [P, HALF], U32)
                 nc.vector.tensor_copy(v[a][h][:], tab[a][:].indirect(entries(idx1, HALF * h, HALF)))
-        nc.vector.tensor_copy(
-            w2_sc[:].rearrange("p t m -> p m t"), w2_sc_raw[:].rearrange("p (m t) -> p m t", t=PACK)
-        )
+        deal_w1(nc.scalar.copy, 1, 0, P // 2, w1_last[:, 0, :, :])
+        deal_w1(nc.vector.tensor_copy, 1, P // 2, P, w1_last[:, 1, :, :])
+        quantise_w1(1)
 
         def first_product(out, a, t, h, j0, count, start, stop):
             nc.tensor.matmul_mx(
@@ -168,13 +171,13 @@ def tile_list_polar_cell_tuning_kernel(
                 pairs[:].rearrange("p u n e -> p u (n e)").bitcast(F32).rearrange("p u n -> p n u"),
             )
 
-        hval = [tile("hval%d" % h, [P, PACK, HALF], F32) for h in range(2)]
+        hval = tile("hval", [P, PACK, S], F32)
 
-        def put(t, h, j0, count):
+        def put(t, j0, count):
             nc.vector.tensor_tensor(
-                page[t][:].indirect(entries(idx2, HALF * h + j0, count)),
-                hval[h][:, t, j0 : j0 + count],
-                wgs_sb[t][:, HALF * h + j0 : HALF * h + j0 + count],
+                page[t][:].indirect(entries(idx2, j0, count)),
+                hval[:, t, j0 : j0 + count],
+                wgs_sb[t][:, j0 : j0 + count],
                 MULT,
             )
 
@@ -190,36 +193,30 @@ def tile_list_polar_cell_tuning_kernel(
         gain_cols = gain_sb[:].unsqueeze(1).to_broadcast([P, BLOCK, PACK])
         bent0, resp0 = [], []
         for c in range(HALF // CHUNK):
-            grouped = tile("bent_bf0_%d" % c, [P, CHUNK, PACK], BF16)
-            for i in range(CHUNK // BLOCK):
-                b = c * (CHUNK // BLOCK) + i
+            grouped = tile("bent_bf0_%d" % c, [P, CHUNK, PACK], BF16, tag="k2", bufs=2)
+            for b in range(2 * c, 2 * c + 2):
                 bentf = tile("tanh0_%d" % b, [P, BLOCK, PACK], F32, tag="f2k", bufs=4)
                 nc.scalar.activation(bentf[:], base0[b][:].rearrange("p t n -> p n t"), ACT.Tanh)
-                nc.vector.tensor_tensor(grouped[:, BLOCK * i : BLOCK * (i + 1), :], bentf[:], gain_cols, MULT)
-            codes, scales = quantise("bent0_%d" % c, grouped, CHUNK)
-            for u in range(2):
-                acc = bank(blocks + 2 * c + u, "resp0_%d_%d" % (c, u), [P, 2, CHUNK])
-                for e in range(2):
-                    second_product(acc[:, e, :], 2 * u + e, codes, scales)
-                resp0.append(acc)
+                nc.vector.tensor_tensor(
+                    grouped[:, BLOCK * (b % 2) : BLOCK * (b % 2 + 1), :], bentf[:], gain_cols, MULT
+                )
+            bent0.append(quantise("bent0_%d" % c, grouped, CHUNK))
         for b in range(blocks):
-            nc.scalar.copy(hval[0][:, :, BLOCK * b : BLOCK * (b + 1)], base0[b][:])
-
-        def respond0(c, u):
-            part = hval[0][:, 2 * u : 2 * u + 2, CHUNK * c : CHUNK * (c + 1)]
-            nc.vector.tensor_tensor(part, resp0[2 * c + u][:], part, MULT)
-
-        respond0(0, 0)
-        respond0(0, 1)
-        put(0, 0, 0, CHUNK)
-        respond0(1, 0)
-        respond0(1, 1)
-        put(0, 0, CHUNK, CHUNK)
+            nc.scalar.copy(hval[:, :, BLOCK * b : BLOCK * (b + 1)], base0[b][:])
+        for c in range(HALF // CHUNK):
+            for u in range(2):
+                acc = bank((4, 0)[c] + u, "resp0_%d_%d" % (c, u), [P, 2, CHUNK])
+                for e in range(2):
+                    second_product(acc[:, e, :], 2 * u + e, *bent0[c])
+                part = hval[:, 2 * u : 2 * u + 2, CHUNK * c : CHUNK * (c + 1)]
+                nc.vector.tensor_tensor(part, acc[:], part, MULT)
+            put(0, CHUNK * c, CHUNK)
+        put(1, 0, HALF)
 
         pairs = tile("bent_pairs", [P, 2, HALF, 2], BF16)
         base1 = []
         for t in range(PACK):
-            acc = bank(t, "base1_%d" % t, [P, HALF])
+            acc = bank((6, 7, 2, 3)[t], "base1_%d" % t, [P, HALF])
             for a in range(passes):
                 first_product(acc[:], a, t, 1, 0, HALF, a == 0, a == passes - 1)
             bentf = tile("tanh1_%d" % t, [P, HALF], F32, tag="f2k", bufs=4)
@@ -229,14 +226,14 @@ def tile_list_polar_cell_tuning_kernel(
         grouped = tile("bent_bf1", [P, HALF, PACK], BF16)
         weave(nc.scalar.copy, grouped, pairs)
         for t in range(PACK):
-            nc.scalar.copy(hval[1][:, t, :], base1[t][:])
+            nc.scalar.copy(hval[:, t, HALF:], base1[t][:])
         codes, scales = quantise("bent1", grouped, HALF)
         resp1 = []
         for t in range(PACK):
-            acc = bank(PACK + t, "resp1_%d" % t, [P, HALF])
+            acc = bank((4, 5, 0, 1)[t], "resp1_%d" % t, [P, HALF])
             second_product(acc[:], t, codes, scales)
             resp1.append(acc)
-        put(1, 0, 0, HALF)
+        put(2, 0, HALF)
 
         w3_bf = tile("w3_bf", [P, N, PACK], BF16)
         nc.scalar.copy(w3_bf[:], w3_raw[:].rearrange("p j c -> p c j"))
@@ -250,37 +247,52 @@ def tile_list_polar_cell_tuning_kernel(
         cols = T2 // 2
         page_pairs = [tile("page_pairs%d" % h, [P, 2, cols, 2], BF16) for h in range(2)]
         x_pairs = [tile("x_pairs%d" % h, [P, 2, HALF, 2], BF16) for h in range(2)]
+        last = PACK - 1
         for t in range(PACK):
-            nc.vector.tensor_tensor(hval[1][:, t, :], resp1[t][:], hval[1][:, t, :], MULT)
-            if t >= 2:
-                put(t, 0, 0, HALF)
-            put(t, 1, 0, HALF)
+            nc.vector.tensor_tensor(hval[:, t, HALF:], resp1[t][:], hval[:, t, HALF:], MULT)
+            if t < last:
+                put(t, HALF, HALF)
+            else:
+                put(t, 0, S)
             nc.sync.dma_start(out1_rows[:, t, :], page[t][:])
+            picked = tile("picked%d" % t, [P, NREAD], F32)
+            step = NREAD if t < last else HALF
+            for j0 in range(0, NREAD, step):
+                nc.vector.tensor_copy(picked[:, j0 : j0 + step], page[t][:].indirect(entries(idx3, j0, step)))
             for h in range(2):
-                picked = tile("picked%d_%d" % (t, h), [P, HALF], F32, tag="picked", bufs=4)
-                nc.vector.tensor_copy(picked[:], page[t][:].indirect(entries(idx3, HALF * h, HALF)))
                 nc.scalar.copy(page_pairs[h][:, t // 2, :, t % 2], page[t][:, cols * h : cols * (h + 1)])
                 nc.scalar.activation(
-                    x_pairs[h][:, t // 2, :, t % 2], picked[:], ACT.Identity, bias=b3_sb[:, t : t + 1]
+                    x_pairs[h][:, t // 2, :, t % 2], picked[:, HALF * h : HALF * (h + 1)], ACT.Identity,
+                    bias=b3_sb[:, t : t + 1],
                 )
 
+        neg_low = tile("neg_low", [P, N // P], F32)
+        nc.scalar.mul(neg_low[:], low_sb[:], -1.0)
         plane_sc = tile("plane_sc", [P, T2], U8)
         out2_words = out_2[0].rearrange("p c i -> p (c i)").bitcast(I32)
-        for h in range(2):
-            engine_copy = nc.vector.tensor_copy if h == 0 else nc.scalar.copy
-            x_bf = tile("x_bf%d" % h, [P, HALF, PACK], BF16, tag="mid4", bufs=2)
-            page_bf = tile("page_bf%d" % h, [P, cols, PACK], BF16, tag="big8", bufs=2)
-            weave(engine_copy, x_bf, x_pairs[h])
-            weave(engine_copy, page_bf, page_pairs[h])
-            codes, scales = quantise("x%d" % h, x_bf, HALF)
+        page_bf = [tile("page_bf%d" % h, [P, cols, PACK], BF16, tag="big8", bufs=2) for h in range(2)]
+
+        def planes(h):
             plane = tile("plane%d" % h, [P, cols], U32)
             nc.vector.quantize_mx(
                 plane[:].bitcast(FP8X4), plane_sc[:, cols * h : cols * (h + 1)],
-                page_bf[:].rearrange("p n t -> p (n t)"),
+                page_bf[h][:].rearrange("p n t -> p (n t)"),
             )
             nc.sync.dma_start(out2_words[:, cols * h : cols * (h + 1)], plane[:].bitcast(I32))
+
+        weave(nc.vector.tensor_copy, page_bf[0], page_pairs[0])
+        weave(nc.scalar.copy, page_bf[1], page_pairs[1])
+        x = []
+        for h in range(2):
+            x_bf = tile("x_bf%d" % h, [P, HALF, PACK], BF16, tag="mid4", bufs=2)
+            weave(nc.vector.tensor_copy, x_bf, x_pairs[h])
+            if h == 0:
+                planes(0)
+            x.append(quantise("x%d" % h, x_bf, HALF))
+        for h in range(2):
+            codes, scales = x[h]
             for u in range(N // P):
-                acc = bank((3 * h + u), "y%d_%d" % (h, u), [P, HALF])
+                acc = bank((6, 7, 2, 3, 4, 5)[3 * h + u], "y%d_%d" % (h, u), [P, HALF])
                 nc.tensor.matmul_mx(
                     acc[:],
                     lhsT=w3_codes[:, P * u : P * (u + 1)].bitcast(FP8X4),
@@ -290,9 +302,16 @@ def tile_list_polar_cell_tuning_kernel(
                     start=True,
                     stop=True,
                 )
-                y = tile("y_sb%d_%d" % (h, u), [P, HALF], F32, tag="f2k", bufs=4)
-                nc.vector.tensor_scalar_max(y[:], acc[:], low_sb[:, u : u + 1])
+                if h == 1 and u >= 1:
+                    y = tile("y_sb%d_%d" % (h, u), [P, HALF], F32, tag="k2", bufs=2)
+                    nc.scalar.activation(y[:], acc[:], ACT.Relu, bias=neg_low[:, u : u + 1])
+                    nc.scalar.activation(y[:], y[:], ACT.Identity, bias=low_sb[:, u : u + 1])
+                else:
+                    y = tile("y_sb%d_%d" % (h, u), [P, HALF], F32, tag="f2k", bufs=4)
+                    nc.vector.tensor_scalar_max(y[:], acc[:], low_sb[:, u : u + 1])
                 nc.sync.dma_start(out_0[P * u : P * (u + 1), HALF * h : HALF * (h + 1)], y[:])
+            if h == 0:
+                planes(1)
         for q in range(4):
             nc.scalar.dma_start(
                 out_3[0, 4 * q : 4 * q + 4, :].bitcast(I32), plane_sc[32 * q : 32 * q + 4, :].bitcast(I32)

@@ -18,9 +18,18 @@ ACT = mybir.ActivationFunctionType
 
 P = 128
 PACK = 4
+QUADRANT = 32
+SCALE_ROWS = 4
+LIST_ROWS = 16
 HALF = 512
 CHUNK = 256
 BLOCK = 128
+QUADRANT_ORDER = (0, 2, 1, 3)
+RESP_FIRST_BANKS = (4, 0)
+BASE_SECOND_BANKS = (6, 7, 2, 3)
+RESP_SECOND_BANKS = (4, 5, 0, 1)
+SCORE_BANKS = (6, 7, 2, 3, 4, 5)
+SCALAR_FLOORED = 2
 
 
 def tile_list_polar_cell_tuning_kernel(
@@ -29,6 +38,8 @@ def tile_list_polar_cell_tuning_kernel(
 ):
     nc = tc.nc
     passes = K // (P * PACK)
+    last = PACK - 1
+    page_half = T2 // 2
     with ExitStack() as ctx:
         sb = ctx.enter_context(tc.tile_pool(name="sb", bufs=1))
         ps = ctx.enter_context(tc.psum_pool(name="ps", bufs=1))
@@ -36,106 +47,113 @@ def tile_list_polar_cell_tuning_kernel(
         def tile(name, shape, dtype, tag="", bufs=1):
             return sb.tile(shape, dtype, name=name, tag=tag or name, bufs=bufs, align_bytes=64)
 
-        def bank(b, name, shape):
-            return ps.tile(shape, F32, name=name, tag="bank%d" % b)
+        def bank(number, name, shape):
+            return ps.tile(shape, F32, name=name, tag="bank%d" % number)
 
-        def entries(lst, j0, count):
-            return lst[:, j0 // 16 : (j0 + count) // 16]
+        def entries(index_tile, j0, count):
+            return index_tile[:, j0 // LIST_ROWS : (j0 + count) // LIST_ROWS]
 
-        idx1 = sb.tile([P, S // 16], U16, name="idx1")
-        idx2 = sb.tile([P, S // 16], U16, name="idx2")
-        idx3 = sb.tile([P, NREAD // 16], U16, name="idx3")
+        def scale_partitions(q, a):
+            first = QUADRANT * q + SCALE_ROWS * a
+            return slice(first, first + SCALE_ROWS)
+
+        def scale_rows(q):
+            return slice(SCALE_ROWS * q, SCALE_ROWS * (q + 1))
+
+        idx1 = sb.tile([P, S // LIST_ROWS], U16, name="idx1")
+        idx2 = sb.tile([P, S // LIST_ROWS], U16, name="idx2")
+        idx3 = sb.tile([P, NREAD // LIST_ROWS], U16, name="idx3")
         nc.sync.dma_start(idx1[:], offs)
 
         tab_sc = tile("tab_sc", [P, T], U8)
         w2_sc_raw = tile("w2_sc_raw", [P, H], U8)
-        nc.vector.memset(tab_sc[:].bitcast(I32), 0)
+        nc.vector.memset(tab_sc[:, : T // 2].bitcast(I32), 0)
+        nc.gpsimd.memset(tab_sc[:, T // 2 :].bitcast(I32), 0)
         nc.vector.memset(w2_sc_raw[:].bitcast(I32), 0)
-        for q in range(4):
-            nc.gpsimd.dma_start(
-                tab_sc[32 * q : 32 * q + 4 * passes, :].bitcast(I32),
-                tab_scales[:, 4 * q : 4 * q + 4, :].bitcast(I32),
-            )
-        for q in range(4):
-            nc.gpsimd.dma_start(
-                w2_sc_raw[32 * q : 32 * q + 4, :].bitcast(I32), w2_scales[0, 4 * q : 4 * q + 4, :].bitcast(I32)
-            )
 
         gain_sb = tile("gain_sb", [P, PACK], F32)
         nc.sync.dma_start(gain_sb[:], gain.rearrange("(p t) -> p t", t=PACK))
         w2_raw = tile("w2_raw", [P, 2 * H], U8)
         nc.sync.dma_start(w2_raw[:].bitcast(I32), w2_words[0].bitcast(I32))
+        nc.sync.dma_start(idx2[:], offs2)
+        b3_sb = tile("b3_sb", [P, PACK], F32)
+        nc.sync.dma_start(b3_sb[:], b3.rearrange("(p t) -> p t", t=PACK))
+        low_sb = tile("low_sb", [P, N // P], F32)
         w1_rows = w1.rearrange("(a p j) c -> a p j c", p=P, j=PACK)
-        w1_first = tile("w1_first", [P, PACK, H], F32, tag="big8", bufs=2)
-        nc.sync.dma_start(w1_first[:], w1_rows[0])
+        w1_raw = [tile("w1_raw%d" % a, [P, PACK, H], F32, tag="wide", bufs=2) for a in range(passes)]
+        for j in range(PACK):
+            nc.sync.dma_start(w1_raw[0][:, j, :], w1_rows[0][:, j, :])
+        for a in range(passes):
+            for q in QUADRANT_ORDER:
+                nc.sync.dma_start(
+                    tab_sc[scale_partitions(q, a), :].bitcast(I32), tab_scales[a, scale_rows(q), :].bitcast(I32)
+                )
+            if a == 0:
+                nc.sync.dma_start(w1_raw[1][:], w1_rows[1])
         tab = []
         for a in range(passes):
             words = tile("tab%d" % a, [P, T], U32)
             nc.sync.dma_start(words[:].bitcast(I32), tab_words[a].rearrange("p c i -> p (c i)").bitcast(I32))
             tab.append(words)
-        w1_last = tile("w1_last", [P, 2, PACK, H // 2], F32, tag="big8", bufs=2)
-        for s in range(2):
-            nc.sync.dma_start(w1_last[:, s, :, :], w1_rows[1][:, :, H // 2 * s : H // 2 * (s + 1)])
-        nc.sync.dma_start(idx2[:], offs2)
+            if a == 0:
+                for q in range(P // QUADRANT):
+                    nc.sync.dma_start(
+                        w2_sc_raw[scale_partitions(q, 0), :].bitcast(I32),
+                        w2_scales[0, scale_rows(q), :].bitcast(I32),
+                    )
 
         wgs_rows = wgs.rearrange("(p t) j -> p t j", t=PACK)
         page_rows = page0.rearrange("(p t) c -> p t c", t=PACK)
         out1_rows = out_1.rearrange("(p t) c -> p t c", t=PACK)
-        wgs_sb, page = [], []
-        b3_sb = tile("b3_sb", [P, PACK], F32)
-        low_sb = tile("low_sb", [P, N // P], F32)
+        page = [tile("page%d" % t, [P, T2], F32) for t in range(PACK)]
+        wgs_sb = tile("wgs_sb", [P, PACK, S], F32)
         w3_raw = tile("w3_raw", [P, PACK, N], F32)
-        for t in range(PACK):
-            factors = tile("wgs%d" % t, [P, S], F32)
-            for q in (0, 2, 1, 3):
-                nc.sync.dma_start(factors[32 * q : 32 * (q + 1), :], wgs_rows[:, t, :])
-            wgs_sb.append(factors)
-            cells = tile("page%d" % t, [P, T2], F32)
-            nc.sync.dma_start(cells[:], page_rows[:, t, :])
-            page.append(cells)
-            if t == 2:
-                nc.sync.dma_start(idx3[:], offs3)
-                nc.sync.dma_start(b3_sb[:], b3.rearrange("(p t) -> p t", t=PACK))
-                with nc.allow_non_contiguous_dma(reason="one floor value a partition"):
-                    nc.sync.dma_start(low_sb[:], low.rearrange("(u p) -> p u", p=P))
-                nc.sync.dma_start(w3_raw[:], w3.rearrange("(p j) c -> p j c", j=PACK))
 
-        warm = tile("warm", [P, 1], F32)
-        nc.vector.memset(warm[:], 0.0)
-        warm_out = tile("warm_out", [P, 1], F32)
-        nc.scalar.activation(warm_out[:], warm[:], ACT.Tanh)
+        def load_page(t):
+            nc.sync.dma_start(page[t][:], page_rows[:, t, :])
+
+        def load_factors(u, h):
+            for q in QUADRANT_ORDER:
+                nc.sync.dma_start(
+                    wgs_sb[QUADRANT * q : QUADRANT * (q + 1), 2 * u : 2 * u + 2, HALF * h : HALF * (h + 1)],
+                    wgs_rows[:, 2 * u : 2 * u + 2, HALF * h : HALF * (h + 1)],
+                )
+
+        load_page(0)
+        load_factors(0, 0)
+        load_page(1)
+        load_factors(1, 0)
+        load_page(2)
+        load_factors(0, 1)
+        nc.sync.dma_start(idx3[:], offs3)
+        nc.sync.dma_start(w3_raw[:], w3.rearrange("(p j) c -> p j c", j=PACK))
+        load_factors(1, 1)
+        load_page(3)
+        with nc.allow_non_contiguous_dma(reason="one floor value a partition"):
+            nc.sync.dma_start(low_sb[:], low.rearrange("(u p) -> p u", p=P))
 
         w2_codes = tile("w2_codes", [P, PACK, P, 2], U8)
         w2_sc = tile("w2_sc", [P, PACK, P], U8)
         nc.vector.tensor_copy(w2_codes[:], w2_raw[:].rearrange("p (m t b) -> p t m b", t=PACK, b=2))
-        w1_bf = [tile("w1_bf%d" % a, [P, PACK, P, PACK], BF16, tag="mid4", bufs=2) for a in range(passes)]
+        w1_bf = [tile("w1_bf%d" % a, [P, PACK, P, PACK], BF16, tag="medium", bufs=2) for a in range(passes)]
         w1_codes = [tile("w1_codes%d" % a, [P, H], U32) for a in range(passes)]
         w1_sc = [tile("w1_sc%d" % a, [P, H], U8) for a in range(passes)]
-
-        def deal_w1(engine_copy, a, m0, m1, raw):
-            engine_copy(
-                w1_bf[a][:, :, m0:m1, :].rearrange("p t m j -> p m t j"),
-                raw.rearrange("p j (m t) -> p m t j", t=PACK),
+        for a in range(passes):
+            nc.scalar.copy(
+                w1_bf[a][:].rearrange("p t m j -> p m t j"), w1_raw[a][:].rearrange("p j (m t) -> p m t j", t=PACK)
             )
-
-        def quantise_w1(a):
             nc.vector.quantize_mx(
                 w1_codes[a][:].bitcast(FP8X4), w1_sc[a][:], w1_bf[a][:].rearrange("p t m j -> p (t m j)")
             )
 
-        deal_w1(nc.scalar.copy, 0, 0, P, w1_first[:])
-        quantise_w1(0)
         v_sc = tile("v_sc", [P, S], U8)
         nc.vector.tensor_copy(v_sc[:], tab_sc[:].indirect(idx1[:]))
-        nc.vector.tensor_copy(w2_sc[:], w2_sc_raw[:].rearrange("p (m t) -> p t m", t=PACK))
-        v = [[None, None] for a in range(passes)]
+        v = [[tile("v%d_%d" % (a, h), [P, HALF], U32) for h in range(2)] for a in range(passes)]
         for a in range(passes):
             for h in range(2):
-                v[a][h] = tile("v%d_%d" % (a, h), [P, HALF], U32)
                 nc.vector.tensor_copy(v[a][h][:], tab[a][:].indirect(entries(idx1, HALF * h, HALF)))
-        deal_w1(nc.scalar.copy, 1, 0, P // 2, w1_last[:, 0, :, :])
-        deal_w1(nc.vector.tensor_copy, 1, P // 2, P, w1_last[:, 1, :, :])
-        quantise_w1(1)
+            if a == 0:
+                nc.vector.tensor_copy(w2_sc[:], w2_sc_raw[:].rearrange("p (m t) -> p t m", t=PACK))
 
         def first_product(out, a, t, h, j0, count, start, stop):
             nc.tensor.matmul_mx(
@@ -143,7 +161,7 @@ def tile_list_polar_cell_tuning_kernel(
                 lhsT=w1_codes[a][:, P * t : P * (t + 1)].bitcast(FP8X4),
                 lhsT_scale=w1_sc[a][:, P * t : P * (t + 1)],
                 rhs=v[a][h][:, j0 : j0 + count].bitcast(FP8X4),
-                rhs_scale=v_sc[4 * a : P, HALF * h + j0 : HALF * h + j0 + count],
+                rhs_scale=v_sc[SCALE_ROWS * a : P, HALF * h + j0 : HALF * h + j0 + count],
                 start=start,
                 stop=stop,
             )
@@ -159,15 +177,15 @@ def tile_list_polar_cell_tuning_kernel(
                 stop=True,
             )
 
-        def quantise(name, grouped, width):
+        def quantise(name, woven, width):
             codes = tile(name + "_codes", [P, width], U32)
             scales = tile(name + "_sc", [P, width], U8)
-            nc.vector.quantize_mx(codes[:].bitcast(FP8X4), scales[:], grouped[:].rearrange("p n t -> p (n t)"))
+            nc.vector.quantize_mx(codes[:].bitcast(FP8X4), scales[:], woven[:].rearrange("p n t -> p (n t)"))
             return codes, scales
 
-        def weave(engine_copy, grouped, pairs):
+        def weave(engine_copy, woven, pairs):
             engine_copy(
-                grouped[:].rearrange("p n t -> p (n t)").bitcast(F32).rearrange("p (n u) -> p n u", u=2),
+                woven[:].rearrange("p n t -> p (n t)").bitcast(F32).rearrange("p (n u) -> p n u", u=2),
                 pairs[:].rearrange("p u n e -> p u (n e)").bitcast(F32).rearrange("p u n -> p n u"),
             )
 
@@ -177,81 +195,89 @@ def tile_list_polar_cell_tuning_kernel(
             nc.vector.tensor_tensor(
                 page[t][:].indirect(entries(idx2, j0, count)),
                 hval[:, t, j0 : j0 + count],
-                wgs_sb[t][:, j0 : j0 + count],
+                wgs_sb[:, t, j0 : j0 + count],
                 MULT,
             )
 
         blocks = HALF // BLOCK
-        base0 = [bank(b, "base0_%d" % b, [P, PACK, BLOCK]) for b in range(blocks)]
+        blocks_in_chunk = CHUNK // BLOCK
+        base_first = [bank(b, "base_first%d" % b, [P, PACK, BLOCK]) for b in range(blocks)]
         for a in range(passes):
             for b in range(blocks):
                 for t in range(PACK):
                     first_product(
-                        base0[b][:, t, :], a, t, 0, BLOCK * b, BLOCK,
-                        a == 0 and t == 0, a == passes - 1 and t == PACK - 1,
+                        base_first[b][:, t, :], a, t, 0, BLOCK * b, BLOCK,
+                        a == 0 and t == 0, a == passes - 1 and t == last,
                     )
         gain_cols = gain_sb[:].unsqueeze(1).to_broadcast([P, BLOCK, PACK])
-        bent0, resp0 = [], []
+        bent_first = []
         for c in range(HALF // CHUNK):
-            grouped = tile("bent_bf0_%d" % c, [P, CHUNK, PACK], BF16, tag="k2", bufs=2)
-            for b in range(2 * c, 2 * c + 2):
-                bentf = tile("tanh0_%d" % b, [P, BLOCK, PACK], F32, tag="f2k", bufs=4)
-                nc.scalar.activation(bentf[:], base0[b][:].rearrange("p t n -> p n t"), ACT.Tanh)
-                nc.vector.tensor_tensor(
-                    grouped[:, BLOCK * (b % 2) : BLOCK * (b % 2 + 1), :], bentf[:], gain_cols, MULT
-                )
-            bent0.append(quantise("bent0_%d" % c, grouped, CHUNK))
+            bent_chunk = tile("bent_chunk%d" % c, [P, CHUNK, PACK], BF16, tag="chunk", bufs=2)
+            for i in range(blocks_in_chunk):
+                b = blocks_in_chunk * c + i
+                tanh_block = tile("tanh_block%d" % b, [P, BLOCK, PACK], F32, tag="bank_copy", bufs=4)
+                nc.scalar.activation(tanh_block[:], base_first[b][:].rearrange("p t n -> p n t"), ACT.Tanh)
+                nc.vector.tensor_tensor(bent_chunk[:, BLOCK * i : BLOCK * (i + 1), :], tanh_block[:], gain_cols, MULT)
+            bent_first.append(quantise("bent_first%d" % c, bent_chunk, CHUNK))
         for b in range(blocks):
-            nc.scalar.copy(hval[:, :, BLOCK * b : BLOCK * (b + 1)], base0[b][:])
+            nc.scalar.copy(hval[:, :, BLOCK * b : BLOCK * (b + 1)], base_first[b][:])
         for c in range(HALF // CHUNK):
             for u in range(2):
-                acc = bank((4, 0)[c] + u, "resp0_%d_%d" % (c, u), [P, 2, CHUNK])
+                resp_pair = bank(RESP_FIRST_BANKS[c] + u, "resp_first%d_%d" % (c, u), [P, 2, CHUNK])
                 for e in range(2):
-                    second_product(acc[:, e, :], 2 * u + e, *bent0[c])
+                    second_product(resp_pair[:, e, :], 2 * u + e, *bent_first[c])
                 part = hval[:, 2 * u : 2 * u + 2, CHUNK * c : CHUNK * (c + 1)]
-                nc.vector.tensor_tensor(part, acc[:], part, MULT)
+                nc.vector.tensor_tensor(part, resp_pair[:], part, MULT)
             put(0, CHUNK * c, CHUNK)
         put(1, 0, HALF)
 
-        pairs = tile("bent_pairs", [P, 2, HALF, 2], BF16)
-        base1 = []
+        bent_pairs = tile("bent_pairs", [P, 2, HALF, 2], BF16)
+        base_second = []
         for t in range(PACK):
-            acc = bank((6, 7, 2, 3)[t], "base1_%d" % t, [P, HALF])
+            base_slice = bank(BASE_SECOND_BANKS[t], "base_second%d" % t, [P, HALF])
             for a in range(passes):
-                first_product(acc[:], a, t, 1, 0, HALF, a == 0, a == passes - 1)
-            bentf = tile("tanh1_%d" % t, [P, HALF], F32, tag="f2k", bufs=4)
-            nc.scalar.activation(bentf[:], acc[:], ACT.Tanh)
-            nc.scalar.activation(pairs[:, t // 2, :, t % 2], bentf[:], ACT.Copy, scale=gain_sb[:, t : t + 1])
-            base1.append(acc)
-        grouped = tile("bent_bf1", [P, HALF, PACK], BF16)
-        weave(nc.scalar.copy, grouped, pairs)
+                first_product(base_slice[:], a, t, 1, 0, HALF, a == 0, a == passes - 1)
+            tanh_slice = tile("tanh_slice%d" % t, [P, HALF], F32, tag="bank_copy", bufs=4)
+            nc.scalar.activation(tanh_slice[:], base_slice[:], ACT.Tanh)
+            nc.scalar.activation(
+                bent_pairs[:, t // 2, :, t % 2], tanh_slice[:], ACT.Copy, scale=gain_sb[:, t : t + 1]
+            )
+            base_second.append(base_slice)
+        bent_half = tile("bent_half", [P, HALF, PACK], BF16)
+        weave(nc.scalar.copy, bent_half, bent_pairs)
         for t in range(PACK):
-            nc.scalar.copy(hval[:, t, HALF:], base1[t][:])
-        codes, scales = quantise("bent1", grouped, HALF)
-        resp1 = []
+            nc.scalar.copy(hval[:, t, HALF:], base_second[t][:])
+        bent_second = quantise("bent_second", bent_half, HALF)
+        resp_second = []
         for t in range(PACK):
-            acc = bank((4, 5, 0, 1)[t], "resp1_%d" % t, [P, HALF])
-            second_product(acc[:], t, codes, scales)
-            resp1.append(acc)
+            resp_slice = bank(RESP_SECOND_BANKS[t], "resp_second%d" % t, [P, HALF])
+            second_product(resp_slice[:], t, *bent_second)
+            resp_second.append(resp_slice)
         put(2, 0, HALF)
 
         w3_bf = tile("w3_bf", [P, N, PACK], BF16)
         nc.scalar.copy(w3_bf[:], w3_raw[:].rearrange("p j c -> p c j"))
         w3_codes = tile("w3_codes", [P, N], U32)
         w3_sc = tile("w3_sc", [P, N], U8)
-        for c0, c1 in ((0, 256), (256, N)):
+        for c0, c1 in ((0, 2 * P), (2 * P, N)):
             nc.vector.quantize_mx(
                 w3_codes[:, c0:c1].bitcast(FP8X4), w3_sc[:, c0:c1], w3_bf[:, c0:c1, :].rearrange("p c j -> p (c j)")
             )
 
-        cols = T2 // 2
-        page_pairs = [tile("page_pairs%d" % h, [P, 2, cols, 2], BF16) for h in range(2)]
+        page_pairs = [tile("page_pairs%d" % h, [P, 2, page_half, 2], BF16) for h in range(2)]
         x_pairs = [tile("x_pairs%d" % h, [P, 2, HALF, 2], BF16) for h in range(2)]
-        last = PACK - 1
+
+        def respond(t):
+            nc.vector.tensor_tensor(hval[:, t, HALF:], resp_second[t][:], hval[:, t, HALF:], MULT)
+
+        def round_page(t, h):
+            nc.scalar.copy(page_pairs[h][:, t // 2, :, t % 2], page[t][:, page_half * h : page_half * (h + 1)])
+
+        respond(0)
         for t in range(PACK):
-            nc.vector.tensor_tensor(hval[:, t, HALF:], resp1[t][:], hval[:, t, HALF:], MULT)
             if t < last:
                 put(t, HALF, HALF)
+                respond(t + 1)
             else:
                 put(t, 0, S)
             nc.sync.dma_start(out1_rows[:, t, :], page[t][:])
@@ -259,60 +285,59 @@ def tile_list_polar_cell_tuning_kernel(
             step = NREAD if t < last else HALF
             for j0 in range(0, NREAD, step):
                 nc.vector.tensor_copy(picked[:, j0 : j0 + step], page[t][:].indirect(entries(idx3, j0, step)))
+            round_page(t, 0)
             for h in range(2):
-                nc.scalar.copy(page_pairs[h][:, t // 2, :, t % 2], page[t][:, cols * h : cols * (h + 1)])
                 nc.scalar.activation(
                     x_pairs[h][:, t // 2, :, t % 2], picked[:, HALF * h : HALF * (h + 1)], ACT.Identity,
                     bias=b3_sb[:, t : t + 1],
                 )
+            round_page(t, 1)
 
         neg_low = tile("neg_low", [P, N // P], F32)
         nc.scalar.mul(neg_low[:], low_sb[:], -1.0)
         plane_sc = tile("plane_sc", [P, T2], U8)
         out2_words = out_2[0].rearrange("p c i -> p (c i)").bitcast(I32)
-        page_bf = [tile("page_bf%d" % h, [P, cols, PACK], BF16, tag="big8", bufs=2) for h in range(2)]
+        page_bf = [tile("page_bf%d" % h, [P, page_half, PACK], BF16, tag="wide", bufs=2) for h in range(2)]
 
         def planes(h):
-            plane = tile("plane%d" % h, [P, cols], U32)
+            columns = slice(page_half * h, page_half * (h + 1))
+            plane = tile("plane%d" % h, [P, page_half], U32)
             nc.vector.quantize_mx(
-                plane[:].bitcast(FP8X4), plane_sc[:, cols * h : cols * (h + 1)],
-                page_bf[h][:].rearrange("p n t -> p (n t)"),
+                plane[:].bitcast(FP8X4), plane_sc[:, columns], page_bf[h][:].rearrange("p n t -> p (n t)")
             )
-            nc.sync.dma_start(out2_words[:, cols * h : cols * (h + 1)], plane[:].bitcast(I32))
+            nc.sync.dma_start(out2_words[:, columns], plane[:].bitcast(I32))
 
+        x_bf = [tile("x_bf%d" % h, [P, HALF, PACK], BF16, tag="medium", bufs=2) for h in range(2)]
         weave(nc.vector.tensor_copy, page_bf[0], page_pairs[0])
         weave(nc.scalar.copy, page_bf[1], page_pairs[1])
-        x = []
+        weave(nc.vector.tensor_copy, x_bf[0], x_pairs[0])
+        planes(0)
+        weave(nc.vector.tensor_copy, x_bf[1], x_pairs[1])
+        x = [quantise("x%d" % h, x_bf[h], HALF) for h in range(2)]
         for h in range(2):
-            x_bf = tile("x_bf%d" % h, [P, HALF, PACK], BF16, tag="mid4", bufs=2)
-            weave(nc.vector.tensor_copy, x_bf, x_pairs[h])
-            if h == 0:
-                planes(0)
-            x.append(quantise("x%d" % h, x_bf, HALF))
-        for h in range(2):
-            codes, scales = x[h]
+            x_codes, x_sc = x[h]
             for u in range(N // P):
-                acc = bank((6, 7, 2, 3, 4, 5)[3 * h + u], "y%d_%d" % (h, u), [P, HALF])
+                score = bank(SCORE_BANKS[(N // P) * h + u], "score%d_%d" % (h, u), [P, HALF])
                 nc.tensor.matmul_mx(
-                    acc[:],
+                    score[:],
                     lhsT=w3_codes[:, P * u : P * (u + 1)].bitcast(FP8X4),
                     lhsT_scale=w3_sc[:, P * u : P * (u + 1)],
-                    rhs=codes[:].bitcast(FP8X4),
-                    rhs_scale=scales[:],
+                    rhs=x_codes[:].bitcast(FP8X4),
+                    rhs_scale=x_sc[:],
                     start=True,
                     stop=True,
                 )
-                if h == 1 and u >= 1:
-                    y = tile("y_sb%d_%d" % (h, u), [P, HALF], F32, tag="k2", bufs=2)
-                    nc.scalar.activation(y[:], acc[:], ACT.Relu, bias=neg_low[:, u : u + 1])
+                if h == 1 and u < SCALAR_FLOORED:
+                    y = tile("y%d_%d" % (h, u), [P, HALF], F32, tag="chunk", bufs=2)
+                    nc.scalar.activation(y[:], score[:], ACT.Relu, bias=neg_low[:, u : u + 1])
                     nc.scalar.activation(y[:], y[:], ACT.Identity, bias=low_sb[:, u : u + 1])
                 else:
-                    y = tile("y_sb%d_%d" % (h, u), [P, HALF], F32, tag="f2k", bufs=4)
-                    nc.vector.tensor_scalar_max(y[:], acc[:], low_sb[:, u : u + 1])
+                    y = tile("y%d_%d" % (h, u), [P, HALF], F32, tag="bank_copy", bufs=4)
+                    nc.vector.tensor_scalar_max(y[:], score[:], low_sb[:, u : u + 1])
                 nc.sync.dma_start(out_0[P * u : P * (u + 1), HALF * h : HALF * (h + 1)], y[:])
             if h == 0:
                 planes(1)
-        for q in range(4):
-            nc.scalar.dma_start(
-                out_3[0, 4 * q : 4 * q + 4, :].bitcast(I32), plane_sc[32 * q : 32 * q + 4, :].bitcast(I32)
-            )
+                for q in range(P // QUADRANT):
+                    nc.sync.dma_start(
+                        out_3[0, scale_rows(q), :].bitcast(I32), plane_sc[scale_partitions(q, 0), :].bitcast(I32)
+                    )

from contextlib import ExitStack

import concourse.mybir as mybir

K, T, S, H, T2, NREAD, N = 1024, 4096, 1024, 512, 2048, 1024, 384
FLOPS = 2 * K * H * S + 2 * H * H * S + 2 * H * N * NREAD

F32 = mybir.dt.float32
BF16 = mybir.dt.bfloat16
I32 = mybir.dt.int32
U32 = mybir.dt.uint32
U16 = mybir.dt.uint16
U8 = mybir.dt.uint8
FP8X4 = mybir.dt.float8_e4m3fn_x4
FP4X4 = mybir.dt.float4_e2m1fn_x4
MULT = mybir.AluOpType.mult
ACT = mybir.ActivationFunctionType

P = 128
PACK = 4
QUADRANT = 32
SCALE_ROWS = 4
LIST_ROWS = 16
HALF = 512
CHUNK = 256
BLOCK = 128
QUADRANT_ORDER = (0, 2, 1, 3)
RESP_FIRST_BANKS = (4, 0)
BASE_SECOND_BANKS = (6, 7, 2, 3)
RESP_SECOND_BANKS = (4, 5, 0, 1)
SCORE_BANKS = (6, 7, 2, 3, 4, 5)
SCALAR_FLOORED = 2


def tile_list_polar_cell_tuning_kernel(
    tc, tab_words, tab_scales, offs, offs2, offs3, w1, gain, w2_words, w2_scales, wgs, page0, b3, w3, low,
    out_0, out_1, out_2, out_3,
):
    nc = tc.nc
    passes = K // (P * PACK)
    last = PACK - 1
    page_half = T2 // 2
    with ExitStack() as ctx:
        sb = ctx.enter_context(tc.tile_pool(name="sb", bufs=1))
        ps = ctx.enter_context(tc.psum_pool(name="ps", bufs=1))

        def tile(name, shape, dtype, tag="", bufs=1):
            return sb.tile(shape, dtype, name=name, tag=tag or name, bufs=bufs, align_bytes=64)

        def bank(number, name, shape):
            return ps.tile(shape, F32, name=name, tag="bank%d" % number)

        def entries(index_tile, j0, count):
            return index_tile[:, j0 // LIST_ROWS : (j0 + count) // LIST_ROWS]

        def scale_partitions(q, a):
            first = QUADRANT * q + SCALE_ROWS * a
            return slice(first, first + SCALE_ROWS)

        def scale_rows(q):
            return slice(SCALE_ROWS * q, SCALE_ROWS * (q + 1))

        idx1 = sb.tile([P, S // LIST_ROWS], U16, name="idx1")
        idx2 = sb.tile([P, S // LIST_ROWS], U16, name="idx2")
        idx3 = sb.tile([P, NREAD // LIST_ROWS], U16, name="idx3")
        nc.sync.dma_start(idx1[:], offs)

        tab_sc = tile("tab_sc", [P, T], U8)
        w2_sc_raw = tile("w2_sc_raw", [P, H], U8)
        nc.vector.memset(tab_sc[:, : T // 2].bitcast(I32), 0)
        nc.gpsimd.memset(tab_sc[:, T // 2 :].bitcast(I32), 0)
        nc.vector.memset(w2_sc_raw[:].bitcast(I32), 0)

        gain_sb = tile("gain_sb", [P, PACK], F32)
        nc.sync.dma_start(gain_sb[:], gain.rearrange("(p t) -> p t", t=PACK))
        w2_raw = tile("w2_raw", [P, 2 * H], U8)
        nc.sync.dma_start(w2_raw[:].bitcast(I32), w2_words[0].bitcast(I32))
        nc.sync.dma_start(idx2[:], offs2)
        b3_sb = tile("b3_sb", [P, PACK], F32)
        nc.sync.dma_start(b3_sb[:], b3.rearrange("(p t) -> p t", t=PACK))
        low_sb = tile("low_sb", [P, N // P], F32)
        w1_rows = w1.rearrange("(a p j) c -> a p j c", p=P, j=PACK)
        w1_raw = [tile("w1_raw%d" % a, [P, PACK, H], F32, tag="wide", bufs=2) for a in range(passes)]
        for j in range(PACK):
            nc.sync.dma_start(w1_raw[0][:, j, :], w1_rows[0][:, j, :])
        for a in range(passes):
            for q in QUADRANT_ORDER:
                nc.sync.dma_start(
                    tab_sc[scale_partitions(q, a), :].bitcast(I32), tab_scales[a, scale_rows(q), :].bitcast(I32)
                )
            if a == 0:
                nc.sync.dma_start(w1_raw[1][:], w1_rows[1])
        tab = []
        for a in range(passes):
            words = tile("tab%d" % a, [P, T], U32)
            nc.sync.dma_start(words[:].bitcast(I32), tab_words[a].rearrange("p c i -> p (c i)").bitcast(I32))
            tab.append(words)
            if a == 0:
                for q in range(P // QUADRANT):
                    nc.sync.dma_start(
                        w2_sc_raw[scale_partitions(q, 0), :].bitcast(I32),
                        w2_scales[0, scale_rows(q), :].bitcast(I32),
                    )

        wgs_rows = wgs.rearrange("(p t) j -> p t j", t=PACK)
        page_rows = page0.rearrange("(p t) c -> p t c", t=PACK)
        out1_rows = out_1.rearrange("(p t) c -> p t c", t=PACK)
        page = [tile("page%d" % t, [P, T2], F32) for t in range(PACK)]
        wgs_sb = tile("wgs_sb", [P, PACK, S], F32)
        w3_raw = tile("w3_raw", [P, PACK, N], F32)

        def load_page(t):
            nc.sync.dma_start(page[t][:], page_rows[:, t, :])

        def load_factors(u, h):
            for q in QUADRANT_ORDER:
                nc.sync.dma_start(
                    wgs_sb[QUADRANT * q : QUADRANT * (q + 1), 2 * u : 2 * u + 2, HALF * h : HALF * (h + 1)],
                    wgs_rows[:, 2 * u : 2 * u + 2, HALF * h : HALF * (h + 1)],
                )

        load_page(0)
        load_factors(0, 0)
        load_page(1)
        load_factors(1, 0)
        load_page(2)
        load_factors(0, 1)
        nc.sync.dma_start(idx3[:], offs3)
        nc.sync.dma_start(w3_raw[:], w3.rearrange("(p j) c -> p j c", j=PACK))
        load_factors(1, 1)
        load_page(3)
        with nc.allow_non_contiguous_dma(reason="one floor value a partition"):
            nc.sync.dma_start(low_sb[:], low.rearrange("(u p) -> p u", p=P))

        w2_codes = tile("w2_codes", [P, PACK, P, 2], U8)
        w2_sc = tile("w2_sc", [P, PACK, P], U8)
        nc.vector.tensor_copy(w2_codes[:], w2_raw[:].rearrange("p (m t b) -> p t m b", t=PACK, b=2))
        w1_bf = [tile("w1_bf%d" % a, [P, PACK, P, PACK], BF16, tag="medium", bufs=2) for a in range(passes)]
        w1_codes = [tile("w1_codes%d" % a, [P, H], U32) for a in range(passes)]
        w1_sc = [tile("w1_sc%d" % a, [P, H], U8) for a in range(passes)]
        for a in range(passes):
            nc.scalar.copy(
                w1_bf[a][:].rearrange("p t m j -> p m t j"), w1_raw[a][:].rearrange("p j (m t) -> p m t j", t=PACK)
            )
            nc.vector.quantize_mx(
                w1_codes[a][:].bitcast(FP8X4), w1_sc[a][:], w1_bf[a][:].rearrange("p t m j -> p (t m j)")
            )

        v_sc = tile("v_sc", [P, S], U8)
        nc.vector.tensor_copy(v_sc[:], tab_sc[:].indirect(idx1[:]))
        v = [[tile("v%d_%d" % (a, h), [P, HALF], U32) for h in range(2)] for a in range(passes)]
        for a in range(passes):
            for h in range(2):
                nc.vector.tensor_copy(v[a][h][:], tab[a][:].indirect(entries(idx1, HALF * h, HALF)))
            if a == 0:
                nc.vector.tensor_copy(w2_sc[:], w2_sc_raw[:].rearrange("p (m t) -> p t m", t=PACK))

        def first_product(out, a, t, h, j0, count, start, stop):
            nc.tensor.matmul_mx(
                out,
                lhsT=w1_codes[a][:, P * t : P * (t + 1)].bitcast(FP8X4),
                lhsT_scale=w1_sc[a][:, P * t : P * (t + 1)],
                rhs=v[a][h][:, j0 : j0 + count].bitcast(FP8X4),
                rhs_scale=v_sc[SCALE_ROWS * a : P, HALF * h + j0 : HALF * h + j0 + count],
                start=start,
                stop=stop,
            )

        def second_product(out, t, codes, scales):
            nc.tensor.matmul_mx(
                out,
                lhsT=w2_codes[:, t, :, :].rearrange("p m b -> p (m b)").bitcast(FP4X4),
                lhsT_scale=w2_sc[:, t, :],
                rhs=codes[:].bitcast(FP8X4),
                rhs_scale=scales[:],
                start=True,
                stop=True,
            )

        def quantise(name, woven, width):
            codes = tile(name + "_codes", [P, width], U32)
            scales = tile(name + "_sc", [P, width], U8)
            nc.vector.quantize_mx(codes[:].bitcast(FP8X4), scales[:], woven[:].rearrange("p n t -> p (n t)"))
            return codes, scales

        def weave(engine_copy, woven, pairs):
            engine_copy(
                woven[:].rearrange("p n t -> p (n t)").bitcast(F32).rearrange("p (n u) -> p n u", u=2),
                pairs[:].rearrange("p u n e -> p u (n e)").bitcast(F32).rearrange("p u n -> p n u"),
            )

        hval = tile("hval", [P, PACK, S], F32)

        def put(t, j0, count):
            nc.vector.tensor_tensor(
                page[t][:].indirect(entries(idx2, j0, count)),
                hval[:, t, j0 : j0 + count],
                wgs_sb[:, t, j0 : j0 + count],
                MULT,
            )

        blocks = HALF // BLOCK
        blocks_in_chunk = CHUNK // BLOCK
        base_first = [bank(b, "base_first%d" % b, [P, PACK, BLOCK]) for b in range(blocks)]
        for a in range(passes):
            for b in range(blocks):
                for t in range(PACK):
                    first_product(
                        base_first[b][:, t, :], a, t, 0, BLOCK * b, BLOCK,
                        a == 0 and t == 0, a == passes - 1 and t == last,
                    )
        gain_cols = gain_sb[:].unsqueeze(1).to_broadcast([P, BLOCK, PACK])
        bent_first = []
        for c in range(HALF // CHUNK):
            bent_chunk = tile("bent_chunk%d" % c, [P, CHUNK, PACK], BF16, tag="chunk", bufs=2)
            for i in range(blocks_in_chunk):
                b = blocks_in_chunk * c + i
                tanh_block = tile("tanh_block%d" % b, [P, BLOCK, PACK], F32, tag="bank_copy", bufs=4)
                nc.scalar.activation(tanh_block[:], base_first[b][:].rearrange("p t n -> p n t"), ACT.Tanh)
                nc.vector.tensor_tensor(bent_chunk[:, BLOCK * i : BLOCK * (i + 1), :], tanh_block[:], gain_cols, MULT)
            bent_first.append(quantise("bent_first%d" % c, bent_chunk, CHUNK))
        for b in range(blocks):
            nc.scalar.copy(hval[:, :, BLOCK * b : BLOCK * (b + 1)], base_first[b][:])
        for c in range(HALF // CHUNK):
            for u in range(2):
                resp_pair = bank(RESP_FIRST_BANKS[c] + u, "resp_first%d_%d" % (c, u), [P, 2, CHUNK])
                for e in range(2):
                    second_product(resp_pair[:, e, :], 2 * u + e, *bent_first[c])
                part = hval[:, 2 * u : 2 * u + 2, CHUNK * c : CHUNK * (c + 1)]
                nc.vector.tensor_tensor(part, resp_pair[:], part, MULT)
            put(0, CHUNK * c, CHUNK)
        put(1, 0, HALF)

        bent_pairs = tile("bent_pairs", [P, 2, HALF, 2], BF16)
        base_second = []
        for t in range(PACK):
            base_slice = bank(BASE_SECOND_BANKS[t], "base_second%d" % t, [P, HALF])
            for a in range(passes):
                first_product(base_slice[:], a, t, 1, 0, HALF, a == 0, a == passes - 1)
            tanh_slice = tile("tanh_slice%d" % t, [P, HALF], F32, tag="bank_copy", bufs=4)
            nc.scalar.activation(tanh_slice[:], base_slice[:], ACT.Tanh)
            nc.scalar.activation(
                bent_pairs[:, t // 2, :, t % 2], tanh_slice[:], ACT.Copy, scale=gain_sb[:, t : t + 1]
            )
            base_second.append(base_slice)
        bent_half = tile("bent_half", [P, HALF, PACK], BF16)
        weave(nc.scalar.copy, bent_half, bent_pairs)
        for t in range(PACK):
            nc.scalar.copy(hval[:, t, HALF:], base_second[t][:])
        bent_second = quantise("bent_second", bent_half, HALF)
        resp_second = []
        for t in range(PACK):
            resp_slice = bank(RESP_SECOND_BANKS[t], "resp_second%d" % t, [P, HALF])
            second_product(resp_slice[:], t, *bent_second)
            resp_second.append(resp_slice)
        put(2, 0, HALF)

        w3_bf = tile("w3_bf", [P, N, PACK], BF16)
        nc.scalar.copy(w3_bf[:], w3_raw[:].rearrange("p j c -> p c j"))
        w3_codes = tile("w3_codes", [P, N], U32)
        w3_sc = tile("w3_sc", [P, N], U8)
        for c0, c1 in ((0, 2 * P), (2 * P, N)):
            nc.vector.quantize_mx(
                w3_codes[:, c0:c1].bitcast(FP8X4), w3_sc[:, c0:c1], w3_bf[:, c0:c1, :].rearrange("p c j -> p (c j)")
            )

        page_pairs = [tile("page_pairs%d" % h, [P, 2, page_half, 2], BF16) for h in range(2)]
        x_pairs = [tile("x_pairs%d" % h, [P, 2, HALF, 2], BF16) for h in range(2)]

        def respond(t):
            nc.vector.tensor_tensor(hval[:, t, HALF:], resp_second[t][:], hval[:, t, HALF:], MULT)

        def round_page(t, h):
            nc.scalar.copy(page_pairs[h][:, t // 2, :, t % 2], page[t][:, page_half * h : page_half * (h + 1)])

        respond(0)
        for t in range(PACK):
            if t < last:
                put(t, HALF, HALF)
                respond(t + 1)
            else:
                put(t, 0, S)
            nc.sync.dma_start(out1_rows[:, t, :], page[t][:])
            picked = tile("picked%d" % t, [P, NREAD], F32)
            step = NREAD if t < last else HALF
            for j0 in range(0, NREAD, step):
                nc.vector.tensor_copy(picked[:, j0 : j0 + step], page[t][:].indirect(entries(idx3, j0, step)))
            round_page(t, 0)
            for h in range(2):
                nc.scalar.activation(
                    x_pairs[h][:, t // 2, :, t % 2], picked[:, HALF * h : HALF * (h + 1)], ACT.Identity,
                    bias=b3_sb[:, t : t + 1],
                )
            round_page(t, 1)

        neg_low = tile("neg_low", [P, N // P], F32)
        nc.scalar.mul(neg_low[:], low_sb[:], -1.0)
        plane_sc = tile("plane_sc", [P, T2], U8)
        out2_words = out_2[0].rearrange("p c i -> p (c i)").bitcast(I32)
        page_bf = [tile("page_bf%d" % h, [P, page_half, PACK], BF16, tag="wide", bufs=2) for h in range(2)]

        def planes(h):
            columns = slice(page_half * h, page_half * (h + 1))
            plane = tile("plane%d" % h, [P, page_half], U32)
            nc.vector.quantize_mx(
                plane[:].bitcast(FP8X4), plane_sc[:, columns], page_bf[h][:].rearrange("p n t -> p (n t)")
            )
            nc.sync.dma_start(out2_words[:, columns], plane[:].bitcast(I32))

        x_bf = [tile("x_bf%d" % h, [P, HALF, PACK], BF16, tag="medium", bufs=2) for h in range(2)]
        weave(nc.vector.tensor_copy, page_bf[0], page_pairs[0])
        weave(nc.scalar.copy, page_bf[1], page_pairs[1])
        weave(nc.vector.tensor_copy, x_bf[0], x_pairs[0])
        planes(0)
        weave(nc.vector.tensor_copy, x_bf[1], x_pairs[1])
        x = [quantise("x%d" % h, x_bf[h], HALF) for h in range(2)]
        for h in range(2):
            x_codes, x_sc = x[h]
            for u in range(N // P):
                score = bank(SCORE_BANKS[(N // P) * h + u], "score%d_%d" % (h, u), [P, HALF])
                nc.tensor.matmul_mx(
                    score[:],
                    lhsT=w3_codes[:, P * u : P * (u + 1)].bitcast(FP8X4),
                    lhsT_scale=w3_sc[:, P * u : P * (u + 1)],
                    rhs=x_codes[:].bitcast(FP8X4),
                    rhs_scale=x_sc[:],
                    start=True,
                    stop=True,
                )
                if h == 1 and u < SCALAR_FLOORED:
                    y = tile("y%d_%d" % (h, u), [P, HALF], F32, tag="chunk", bufs=2)
                    nc.scalar.activation(y[:], score[:], ACT.Relu, bias=neg_low[:, u : u + 1])
                    nc.scalar.activation(y[:], y[:], ACT.Identity, bias=low_sb[:, u : u + 1])
                else:
                    y = tile("y%d_%d" % (h, u), [P, HALF], F32, tag="bank_copy", bufs=4)
                    nc.vector.tensor_scalar_max(y[:], score[:], low_sb[:, u : u + 1])
                nc.sync.dma_start(out_0[P * u : P * (u + 1), HALF * h : HALF * (h + 1)], y[:])
            if h == 0:
                planes(1)
                for q in range(P // QUADRANT):
                    nc.sync.dma_start(
                        out_3[0, scale_rows(q), :].bitcast(I32), plane_sc[scale_partitions(q, 0), :].bitcast(I32)
                    )
